import numpy as np
import ml_dtypes


def mxq(x, axis, fmt="e4m3"):
    dtype, down = {"e4m3": (ml_dtypes.float8_e4m3fn, 7), "e5m2": (ml_dtypes.float8_e5m2, 14)}[fmt]
    v = np.moveaxis(np.asarray(x, np.float32).astype(ml_dtypes.bfloat16).astype(np.float64), axis, -1)
    blocks = v.reshape(v.shape[:-1] + (-1, 32))
    amax = np.abs(blocks).max(-1, keepdims=True)
    byte = np.maximum(np.where(amax > 0, np.frexp(amax)[1] - 1 + 127, 0) - down, 1)
    scale = np.exp2(byte - 127.0)
    codes = (blocks / scale).astype(np.float32).astype(dtype).astype(np.float64)
    return np.moveaxis((codes * scale).reshape(v.shape), -1, axis)


WIDE = False


def mx_kscale(k):
    if not WIDE:
        return np.ones(k)
    levels = np.array([10, -10, 5, -5, 0])
    if k % 512:
        return np.exp2(np.random.permutation(np.resize(levels, k // 32))).repeat(32)
    a = np.empty((k // 512, 16))
    for p in range(k // 512):
        a[p, :8] = np.random.permutation(np.resize(levels, 8))
        for g in range(8):
            far = levels[np.abs(levels - a[p, g]) >= 10]
            a[p, g + 8] = far[np.random.randint(len(far))]
    return np.exp2(a.ravel()).repeat(32)


def f64(x):
    return np.asarray(x).astype(np.float64)


def striped(idx):
    return np.tile(idx.reshape(-1, 16).T, (8, 1)).astype(np.uint16)


def unstriped(offs):
    return offs[:16].T.reshape(-1).astype(np.int64)


def gelu(v):
    return 0.5 * v * (1.0 + np.tanh(np.sqrt(2.0 / np.pi) * (v + 0.044715 * v**3)))


K, T, S, H, N = 1024, 1024, 512, 512, 256
P = 2 ** 7


def setup_inputs():
    n = np.random.standard_normal
    s = mx_kscale(K)[:, None]
    u = mx_kscale(H)
    return {
        "xT": (n((K, T)) * s).astype(np.float32),
        "w1": (n((K, H)) / np.sqrt(K) / s * u).astype(np.float32),
        "w2": (n((H, N)) / np.sqrt(H) / u[:, None]).astype(np.float32),
        "lam": np.tile(np.random.uniform(0.1, 0.9, S), (P, 1)).astype(np.float32),
        "mu": np.tile(np.random.uniform(0.1, 0.9, S), (P, 1)).astype(np.float32),
        "offs": striped(np.random.permutation(T)[:S]),
        "pos1": striped(np.random.permutation(S)),
    }


def reference(xT, w1, w2, lam, mu, offs, pos1):
    xq = mxq(f64(xT)[:, unstriped(offs)], 0, "e4m3")
    h = gelu(mxq(f64(w1), 0, "e4m3").T @ xq)
    z = h * f64(lam)[:1] + h[:, unstriped(pos1)] * f64(mu)[:1]
    return mxq(f64(w2), 0, "e4m3").T @ mxq(z, 0, "e4m3")

@@ -1,0 +1,169 @@
+from contextlib import ExitStack
+
+import concourse.mybir as mybir
+from concourse.masks import make_identity
+
+K, T, S, H, N = 1024, 1024, 512, 512, 256
+P = 128
+F32 = mybir.dt.float32
+BF16 = mybir.dt.bfloat16
+U32 = mybir.dt.uint32
+U16 = mybir.dt.uint16
+U8 = mybir.dt.uint8
+FP8X4 = mybir.dt.float8_e4m3fn_x4
+ACT = mybir.ActivationFunctionType
+ALU = mybir.AluOpType
+FLOPS = 2 * K * H * S + 2 * H * N * S
+
+
+def tile_picked_mixup_gelu_e_kernel(tc, xT, w1, w2, lam, mu, offs, pos1, out):
+    nc = tc.nc
+    with ExitStack() as ctx:
+        keep = ctx.enter_context(tc.tile_pool(name="keep", bufs=1))
+        psum = ctx.enter_context(tc.psum_pool(name="psum", bufs=1))
+
+        def quantize(name, grouped, width):
+            codes = keep.tile([P, width], U32, name=name + "_codes", align_bytes=64)
+            scales = keep.tile([P, width], U8, name=name + "_scales", align_bytes=64)
+            nc.vector.quantize_mx(out=codes[:].bitcast(FP8X4), scales=scales[:], in_=grouped)
+            return codes, scales
+
+        offs_sb = keep.tile([P, S // 16], U16, name="offs_sb")
+        nc.sync.dma_start(offs_sb[:], offs)
+        x_rows = xT.rearrange("(z p j) t -> z j p t", z=2, j=4)
+        w1_rows = w1.rearrange("(z p j) (a c) -> a z p j c", z=2, j=4, a=2)
+        x_planes = []
+        w1_raw = {}
+
+        def load_w1(a, z):
+            w1_raw[a, z] = keep.tile([P, 4, 256], F32, name="w1_raw%d%d" % (a, z))
+            nc.sync.dma_start(w1_raw[a, z][:], w1_rows[a, z])
+
+        for z in range(2):
+            for j in range(4):
+                if (z, j) == (1, 2):
+                    load_w1(0, 0)
+                plane = keep.tile([P, T], F32, name="x_plane%d%d" % (z, j))
+                nc.sync.dma_start(plane[:], x_rows[z, j])
+                x_planes.append(plane)
+        load_w1(0, 1)
+        load_w1(1, 0)
+        load_w1(1, 1)
+        pos_sb = keep.tile([P, S // 16], U16, name="pos_sb")
+        nc.sync.dma_start(pos_sb[:], pos1)
+        lam_col = keep.tile([P, 4], F32, name="lam_col")
+        mu_col = keep.tile([P, 4], F32, name="mu_col")
+        with nc.allow_non_contiguous_dma(reason="one value a partition"):
+            nc.sync.dma_start(lam_col[:], lam[0].rearrange("(b p) -> p b", p=P))
+            nc.sync.dma_start(mu_col[:], mu[0].rearrange("(b p) -> p b", p=P))
+        w2_raw = keep.tile([P, 4, N], F32, name="w2_raw")
+        nc.sync.dma_start(w2_raw[:], w2.rearrange("(p j) n -> p j n", j=4))
+
+        warm = keep.tile([P, 1], F32, name="warm")
+        nc.gpsimd.memset(warm[:], 0.0)
+        warm_out = keep.tile([P, 1], F32, name="warm_out")
+        nc.scalar.activation(warm_out[:], warm[:], ACT.Gelu_apprx_tanh)
+        ident = keep.tile([P, P], F32, name="ident")
+        make_identity(nc, ident[:])
+
+        w1_grouped = {}
+        w1_q = {}
+
+        def cast_w1(a, z, copy):
+            w1_grouped[a, z] = keep.tile([P, 1024], BF16, name="w1_grouped%d%d" % (a, z), tag="w1_grouped%d" % z, align_bytes=64)
+            copy(w1_grouped[a, z][:].rearrange("p (c i j) -> p c j i", i=4, j=4),
+                 w1_raw[a, z][:].rearrange("p j (c i) -> p c j i", i=4))
+
+        def quant_w1(a, z):
+            w1_q[a, z] = quantize("w1%d%d" % (a, z), w1_grouped[a, z][:], 256)
+
+        picked = [keep.tile([P, 4, S], BF16, name="picked%d" % z) for z in range(2)]
+        x_grouped = [keep.tile([P, S * 4], BF16, name="x_grouped%d" % z, align_bytes=64) for z in range(2)]
+
+        def weave(z, lo, hi, copy):
+            src = picked[z][:].rearrange("p j (c i) -> p c j i", i=4)
+            dst = x_grouped[z][:].rearrange("p (c i j) -> p c j i", i=4, j=4)
+            copy(dst[:, lo:hi], src[:, lo:hi])
+
+        x_plane_bf16 = keep.tile([P, T], BF16, name="x_plane_bf16")
+        nc.scalar.copy(x_plane_bf16[:], x_planes[1][:])
+        nc.scalar.activation(picked[0][:, 1, :], x_plane_bf16[:].indirect(offs_sb[:]), ACT.Copy)
+        for j in (0, 2, 3):
+            nc.vector.tensor_copy(picked[0][:, j, :], x_planes[j][:].indirect(offs_sb[:]))
+        weave(0, 0, 128, nc.scalar.copy)
+        cast_w1(0, 0, nc.scalar.copy)
+        for j in range(3):
+            nc.vector.tensor_copy(picked[1][:, j, :], x_planes[4 + j][:].indirect(offs_sb[:]))
+        nc.vector.tensor_copy(picked[1][:, 3, 0:256], x_planes[7][:].indirect(offs_sb[:, 0:16]))
+        weave(1, 0, 32, nc.scalar.copy)
+        nc.vector.tensor_copy(picked[1][:, 3, 256:512], x_planes[7][:].indirect(offs_sb[:, 16:32]))
+        x_q = [quantize("x0", x_grouped[0][:], S)]
+        quant_w1(0, 0)
+        weave(1, 32, 128, nc.vector.tensor_copy)
+        cast_w1(0, 1, nc.scalar.copy)
+        x_q.append(quantize("x1", x_grouped[1][:], S))
+        quant_w1(0, 1)
+        cast_w1(1, 0, nc.scalar.copy)
+        cast_w1(1, 1, nc.vector.tensor_copy)
+        quant_w1(1, 0)
+        quant_w1(1, 1)
+
+        order = [0, 1, 2, 3]
+        h = {}
+        pre = {t: psum.tile([P, S], F32, name="pre%d" % t, tag="bank%d" % t) for t in order}
+
+        def first_product(t, z):
+            a, cols = t // 2, slice(128 * (t % 2), 128 * (t % 2 + 1))
+            nc.tensor.matmul_mx(pre[t][:], lhsT=w1_q[a, z][0][:, cols].bitcast(FP8X4), lhsT_scale=w1_q[a, z][1][:, cols],
+                                rhs=x_q[z][0][:].bitcast(FP8X4), rhs_scale=x_q[z][1][:], start=(z == 0), stop=(z == 1))
+
+        for a in range(2):
+            for z in range(2):
+                first_product(2 * a, z)
+                first_product(2 * a + 1, z)
+        for t in order:
+            h[t] = keep.tile([P, S], F32, name="h%d" % t)
+            nc.scalar.activation(h[t][:], pre[t][:], ACT.Gelu_apprx_tanh)
+
+        probe = keep.tile([P, 2], F32, name="probe")
+        nc.gpsimd.tensor_copy(probe[:, 0:1], h[0][:, 0:1])
+        w2_grouped = keep.tile([P, 4 * N], BF16, name="w2_grouped", align_bytes=64)
+        nc.scalar.copy(w2_grouped[:].rearrange("p (c i j) -> p c j i", i=4, j=4), w2_raw[:].rearrange("p j (c i) -> p c j i", i=4))
+
+        own_t = [psum.tile([P, 4, P], F32, name="own_t%d" % b, tag="bank%d" % (4 + b)) for b in range(4)]
+        for t in order:
+            for b in range(4):
+                nc.tensor.transpose(own_t[b][:, t, :], h[t][:, P * b : P * (b + 1)], ident[:])
+        own = []
+        for b in range(4):
+            scaled = keep.tile([P, H], F32, name="own%d" % b)
+            nc.scalar.activation(scaled[:], own_t[b][:].rearrange("p t m -> p (t m)"), ACT.Copy, scale=lam_col[:, b : b + 1])
+            own.append(scaled)
+        partner_t = [psum.tile([P, 4, P], F32, name="partner_t%d" % b, tag="bank%d" % order[b]) for b in range(4)]
+        for t in order:
+            for half in range(2):
+                partner = keep.tile([P, 256], F32, name="partner%d%d" % (t, half))
+                nc.vector.tensor_copy(partner[:], h[t][:].indirect(pos_sb[:, 16 * half : 16 * (half + 1)]))
+                for r in range(2):
+                    nc.tensor.transpose(partner_t[2 * half + r][:, t, :], partner[:, P * r : P * (r + 1)], ident[:])
+        nc.gpsimd.tensor_copy(probe[:, 1:2], partner[:, 0:1])
+        w2_q = quantize("w2", w2_grouped[:], N)
+
+        out_rows = out.rearrange("(m p) s -> p m s", p=P)
+        for b in range(4):
+            z_t = keep.tile([P, H], BF16, name="z_t%d" % b)
+            nc.vector.scalar_tensor_tensor(z_t[:], partner_t[b][:].rearrange("p t m -> p (t m)"), mu_col[:, b : b + 1], own[b][:], ALU.mult, ALU.add)
+            z_words = psum.tile([P, 2, P], F32, name="z_words%d" % b, tag="bank%d" % (4 + b))
+            for u in range(2):
+                nc.tensor.transpose(z_words[:, u, :], z_t[:].bitcast(F32)[:, u : 2 * P : 2], ident[:])
+            z_grouped = keep.tile([P, 4 * P], BF16, name="z_grouped%d" % b, align_bytes=64)
+            nc.scalar.copy(z_grouped[:].bitcast(F32).rearrange("p (s u) -> p s u", u=2), z_words[:].rearrange("p u s -> p s u"))
+            z_q = quantize("z%d" % b, z_grouped[:], P)
+            acc = psum.tile([P, 2, P], F32, name="acc%d" % b, tag="bank%d" % order[b])
+            for m in range(2):
+                cols = slice(P * m, P * (m + 1))
+                nc.tensor.matmul_mx(acc[:, m, :], lhsT=w2_q[0][:, cols].bitcast(FP8X4), lhsT_scale=w2_q[1][:, cols],
+                                    rhs=z_q[0][:].bitcast(FP8X4), rhs_scale=z_q[1][:], start=True, stop=True)
+            result = keep.tile([P, 2, P], F32, name="result%d" % b)
+            nc.scalar.copy(result[:], acc[:])
+            nc.sync.dma_start(out_rows[:, :, P * b : P * (b + 1)], result[:])

@@ -22,42 +22,57 @@ def tile_picked_mixup_gelu_e_kernel(tc, xT, w1, w2, lam, mu, offs, pos1, out):
         keep = ctx.enter_context(tc.tile_pool(name="keep", bufs=1))
         psum = ctx.enter_context(tc.psum_pool(name="psum", bufs=1))
 
-        def quantize(name, grouped, width):
-            codes = keep.tile([P, width], U32, name=name + "_codes", align_bytes=64)
+        def quantize(name, grouped, width, tag=None):
+            codes = keep.tile([P, width], U32, name=name + "_codes", tag=tag or name + "_codes", align_bytes=64)
             scales = keep.tile([P, width], U8, name=name + "_scales", align_bytes=64)
             nc.vector.quantize_mx(out=codes[:].bitcast(FP8X4), scales=scales[:], in_=grouped)
             return codes, scales
 
         offs_sb = keep.tile([P, S // 16], U16, name="offs_sb")
-        nc.sync.dma_start(offs_sb[:], offs)
-        x_rows = xT.rearrange("(z p j) t -> z j p t", z=2, j=4)
-        w1_rows = w1.rearrange("(z p j) (a c) -> a z p j c", z=2, j=4, a=2)
-        x_planes = []
-        w1_raw = {}
-
-        def load_w1(a, z):
-            w1_raw[a, z] = keep.tile([P, 4, 256], F32, name="w1_raw%d%d" % (a, z))
-            nc.sync.dma_start(w1_raw[a, z][:], w1_rows[a, z])
-
-        for z in range(2):
-            for j in range(4):
-                if (z, j) == (1, 2):
-                    load_w1(0, 0)
-                plane = keep.tile([P, T], F32, name="x_plane%d%d" % (z, j))
-                nc.sync.dma_start(plane[:], x_rows[z, j])
-                x_planes.append(plane)
-        load_w1(0, 1)
-        load_w1(1, 0)
-        load_w1(1, 1)
         pos_sb = keep.tile([P, S // 16], U16, name="pos_sb")
-        nc.sync.dma_start(pos_sb[:], pos1)
         lam_col = keep.tile([P, 4], F32, name="lam_col")
         mu_col = keep.tile([P, 4], F32, name="mu_col")
-        with nc.allow_non_contiguous_dma(reason="one value a partition"):
-            nc.sync.dma_start(lam_col[:], lam[0].rearrange("(b p) -> p b", p=P))
-            nc.sync.dma_start(mu_col[:], mu[0].rearrange("(b p) -> p b", p=P))
         w2_raw = keep.tile([P, 4, N], F32, name="w2_raw")
+        x_rows = xT.rearrange("(z p j) t -> z j p t", z=2, j=4)
+        x_planes = {}
+        w1_raw = {}
+
+        def load_x(n):
+            x_planes[n] = keep.tile([P, T], F32, name="x_plane%d" % n)
+            nc.sync.dma_start(x_planes[n][:], x_rows[n // 4, n % 4])
+
+        def load_w1_half(a, z):
+            raw = keep.tile([P, 4, 256], F32, name="w1_raw%d%d" % (a, z))
+            nc.sync.dma_start(raw[:], w1.rearrange("(z p j) (a c) -> a z p j c", z=2, j=4, a=2)[a, z])
+            w1_raw[a, z] = raw[:]
+
+        def load_w1_pass(z):
+            raw = keep.tile([P, 4, 512], F32, name="w1_raw%d" % z)
+            nc.sync.dma_start(raw[:], w1.rearrange("(z p j) c -> z p j c", z=2, j=4)[z])
+            for a in range(2):
+                w1_raw[a, z] = raw[:, :, 256 * a : 256 * (a + 1)]
+
+        def load_shares():
+            with nc.allow_non_contiguous_dma(reason="one value a partition"):
+                nc.sync.dma_start(lam_col[:], lam[0].rearrange("(b p) -> p b", p=P))
+                nc.sync.dma_start(mu_col[:], mu[0].rearrange("(b p) -> p b", p=P))
+
+        nc.sync.dma_start(offs_sb[:], offs)
+        load_x(0)
+        load_x(1)
+        load_x(2)
+        load_x(3)
+        load_x(4)
+        load_x(5)
+        load_x(6)
+        load_x(7)
+        load_w1_half(0, 0)
+        load_w1_half(0, 1)
+        load_w1_half(1, 0)
+        load_w1_half(1, 1)
+        nc.sync.dma_start(pos_sb[:], pos1)
         nc.sync.dma_start(w2_raw[:], w2.rearrange("(p j) n -> p j n", j=4))
+        load_shares()
 
         warm = keep.tile([P, 1], F32, name="warm")
         nc.gpsimd.memset(warm[:], 0.0)
@@ -65,19 +80,38 @@ def tile_picked_mixup_gelu_e_kernel(tc, xT, w1, w2, lam, mu, offs, pos1, out):
         nc.scalar.activation(warm_out[:], warm[:], ACT.Gelu_apprx_tanh)
         ident = keep.tile([P, P], F32, name="ident")
         make_identity(nc, ident[:])
+        on_scalar, on_vector, on_gpsimd = nc.scalar.copy, nc.vector.tensor_copy, nc.gpsimd.tensor_copy
 
-        w1_grouped = {}
-        w1_q = {}
+        w1_grouped, w1_q, x_q, h, own, z_grouped, w2_state = {}, {}, {}, {}, {}, {}, {}
 
-        def cast_w1(a, z, copy):
-            w1_grouped[a, z] = keep.tile([P, 1024], BF16, name="w1_grouped%d%d" % (a, z), tag="w1_grouped%d" % z, align_bytes=64)
-            copy(w1_grouped[a, z][:].rearrange("p (c i j) -> p c j i", i=4, j=4),
-                 w1_raw[a, z][:].rearrange("p j (c i) -> p c j i", i=4))
+        def cast_w1(t, z, copy):
+            if t not in w1_grouped:
+                w1_grouped[t] = keep.tile([P, 2, 4 * P], BF16, name="w1_grouped%d" % t, tag="w1_grouped%d" % t, align_bytes=64)
+            src = w1_raw[t // 2, z][:, :, P * (t % 2) : P * (t % 2 + 1)]
+            copy(w1_grouped[t][:, z, :].rearrange("p (c i j) -> p c j i", i=4, j=4), src.rearrange("p j (c i) -> p c j i", i=4))
 
-        def quant_w1(a, z):
-            w1_q[a, z] = quantize("w1%d%d" % (a, z), w1_grouped[a, z][:], 256)
+        def quant_w1(t):
+            codes, scales = quantize("w1%d" % t, w1_grouped[t][:].rearrange("p z w -> p (z w)"), 2 * P)
+            for z in range(2):
+                w1_q[t, z] = (codes[:, P * z : P * (z + 1)], scales[:, P * z : P * (z + 1)])
 
-        picked = [keep.tile([P, 4, S], BF16, name="picked%d" % z) for z in range(2)]
+        def quant_w1_pass(t, z):
+            codes, scales = quantize("w1%d%d" % (t, z), w1_grouped[t][:, z, :], P)
+            w1_q[t, z] = (codes[:], scales[:])
+
+        def hidden(t):
+            first_product(t, 0)
+            first_product(t, 1)
+            gelu(t)
+
+        def cast_w2(copy, tag):
+            w2_state["grouped"] = keep.tile([P, 4 * N], BF16, name="w2_grouped", tag=tag, align_bytes=64)
+            copy(w2_state["grouped"][:].rearrange("p (c i j) -> p c j i", i=4, j=4), w2_raw[:].rearrange("p j (c i) -> p c j i", i=4))
+
+        def quant_w2():
+            w2_state["q"] = quantize("w2", w2_state["grouped"][:], N)
+
+        picked = [keep.tile([P, 4, S], BF16, name="picked%d" % z, align_bytes=64) for z in range(2)]
         x_grouped = [keep.tile([P, S * 4], BF16, name="x_grouped%d" % z, align_bytes=64) for z in range(2)]
 
         def weave(z, lo, hi, copy):
@@ -85,85 +119,128 @@ def tile_picked_mixup_gelu_e_kernel(tc, xT, w1, w2, lam, mu, offs, pos1, out):
             dst = x_grouped[z][:].rearrange("p (c i j) -> p c j i", i=4, j=4)
             copy(dst[:, lo:hi], src[:, lo:hi])
 
-        x_plane_bf16 = keep.tile([P, T], BF16, name="x_plane_bf16")
-        nc.scalar.copy(x_plane_bf16[:], x_planes[1][:])
-        nc.scalar.activation(picked[0][:, 1, :], x_plane_bf16[:].indirect(offs_sb[:]), ACT.Copy)
-        for j in (0, 2, 3):
-            nc.vector.tensor_copy(picked[0][:, j, :], x_planes[j][:].indirect(offs_sb[:]))
-        weave(0, 0, 128, nc.scalar.copy)
-        cast_w1(0, 0, nc.scalar.copy)
-        for j in range(3):
-            nc.vector.tensor_copy(picked[1][:, j, :], x_planes[4 + j][:].indirect(offs_sb[:]))
-        nc.vector.tensor_copy(picked[1][:, 3, 0:256], x_planes[7][:].indirect(offs_sb[:, 0:16]))
-        weave(1, 0, 32, nc.scalar.copy)
-        nc.vector.tensor_copy(picked[1][:, 3, 256:512], x_planes[7][:].indirect(offs_sb[:, 16:32]))
-        x_q = [quantize("x0", x_grouped[0][:], S)]
-        quant_w1(0, 0)
-        weave(1, 32, 128, nc.vector.tensor_copy)
-        cast_w1(0, 1, nc.scalar.copy)
-        x_q.append(quantize("x1", x_grouped[1][:], S))
-        quant_w1(0, 1)
-        cast_w1(1, 0, nc.scalar.copy)
-        cast_w1(1, 1, nc.vector.tensor_copy)
-        quant_w1(1, 0)
-        quant_w1(1, 1)
+        def pick(n, lo, hi):
+            nc.vector.tensor_copy(picked[n // 4][:, n % 4, 16 * lo : 16 * hi], x_planes[n][:].indirect(offs_sb[:, lo:hi]))
 
-        order = [0, 1, 2, 3]
-        h = {}
-        pre = {t: psum.tile([P, S], F32, name="pre%d" % t, tag="bank%d" % t) for t in order}
+        def pick_on_scalar(n):
+            rounded = keep.tile([P, T], BF16, name="x_rounded%d" % n)
+            nc.scalar.copy(rounded[:], x_planes[n][:])
+            nc.scalar.activation(picked[n // 4][:, n % 4, :], rounded[:].indirect(offs_sb[:]), ACT.Copy)
+
+        def quant_x(z):
+            x_q[z] = quantize("x%d" % z, x_grouped[z][:], S)
+
+        pre = [psum.tile([P, S], F32, name="pre%d" % t, tag="bank%d" % t) for t in range(4)]
+        own_t = [psum.tile([P, 4, P], F32, name="own_t%d" % b, tag="bank%d" % (4 + b)) for b in range(4)]
+        partner_t = {}
 
         def first_product(t, z):
-            a, cols = t // 2, slice(128 * (t % 2), 128 * (t % 2 + 1))
-            nc.tensor.matmul_mx(pre[t][:], lhsT=w1_q[a, z][0][:, cols].bitcast(FP8X4), lhsT_scale=w1_q[a, z][1][:, cols],
+            nc.tensor.matmul_mx(pre[t][:], lhsT=w1_q[t, z][0].bitcast(FP8X4), lhsT_scale=w1_q[t, z][1],
                                 rhs=x_q[z][0][:].bitcast(FP8X4), rhs_scale=x_q[z][1][:], start=(z == 0), stop=(z == 1))
 
-        for a in range(2):
-            for z in range(2):
-                first_product(2 * a, z)
-                first_product(2 * a + 1, z)
-        for t in order:
-            h[t] = keep.tile([P, S], F32, name="h%d" % t)
+        def gelu(t, tag=None):
+            h[t] = keep.tile([P, S], F32, name="h%d" % t, tag=tag or "h%d" % t)
             nc.scalar.activation(h[t][:], pre[t][:], ACT.Gelu_apprx_tanh)
 
-        probe = keep.tile([P, 2], F32, name="probe")
-        nc.gpsimd.tensor_copy(probe[:, 0:1], h[0][:, 0:1])
-        w2_grouped = keep.tile([P, 4 * N], BF16, name="w2_grouped", align_bytes=64)
-        nc.scalar.copy(w2_grouped[:].rearrange("p (c i j) -> p c j i", i=4, j=4), w2_raw[:].rearrange("p j (c i) -> p c j i", i=4))
-
-        own_t = [psum.tile([P, 4, P], F32, name="own_t%d" % b, tag="bank%d" % (4 + b)) for b in range(4)]
-        for t in order:
+        def turn_own(t):
             for b in range(4):
                 nc.tensor.transpose(own_t[b][:, t, :], h[t][:, P * b : P * (b + 1)], ident[:])
-        own = []
-        for b in range(4):
-            scaled = keep.tile([P, H], F32, name="own%d" % b)
-            nc.scalar.activation(scaled[:], own_t[b][:].rearrange("p t m -> p (t m)"), ACT.Copy, scale=lam_col[:, b : b + 1])
-            own.append(scaled)
-        partner_t = [psum.tile([P, 4, P], F32, name="partner_t%d" % b, tag="bank%d" % order[b]) for b in range(4)]
-        for t in order:
-            for half in range(2):
-                partner = keep.tile([P, 256], F32, name="partner%d%d" % (t, half))
-                nc.vector.tensor_copy(partner[:], h[t][:].indirect(pos_sb[:, 16 * half : 16 * (half + 1)]))
-                for r in range(2):
-                    nc.tensor.transpose(partner_t[2 * half + r][:, t, :], partner[:, P * r : P * (r + 1)], ident[:])
-        nc.gpsimd.tensor_copy(probe[:, 1:2], partner[:, 0:1])
-        w2_q = quantize("w2", w2_grouped[:], N)
+
+        def scale_own(b):
+            own[b] = keep.tile([P, 2, 128, 2], F32, name="own%d" % b, tag="own%d" % b, align_bytes=64)
+            nc.scalar.activation(own[b][:], own_t[b][:].rearrange("s t (p u e) -> s u (t p) e", u=2, e=2), ACT.Copy, scale=lam_col[:, b : b + 1])
+
+        partners = {}
+
+        def fetch_partner(t, lo, hi, tag):
+            if t not in partners:
+                partners[t] = keep.tile([P, S], F32, name="partner%d" % t, tag=tag or "partner%d" % t, align_bytes=64)
+            partner = partners[t][:, P * lo : P * hi]
+            nc.vector.tensor_copy(partner, h[t][:].indirect(pos_sb[:, 8 * lo : 8 * hi]))
+            for b in range(lo, hi):
+                if b not in partner_t:
+                    partner_t[b] = psum.tile([P, 4, P], F32, name="partner_t%d" % b, tag="bank%d" % b)
+                nc.tensor.transpose(partner_t[b][:, t, :], partner[:, P * (b - lo) : P * (b - lo + 1)], ident[:])
+
+        def mix(b, first, width, copy):
+            if first not in z_grouped:
+                z_grouped[first] = keep.tile([P, 4 * width], BF16, name="z_grouped%d" % first, align_bytes=64)
+            z_t = keep.tile([P, 2, 128, 2], BF16, name="z_t%d" % b)
+            z_words = psum.tile([P, 2, P], F32, name="z_words%d" % b, tag="bank%d" % (4 + b))
+            fetched = partner_t[b][:].rearrange("s t (p u e) -> s u (t p) e", u=2, e=2)
+            for u in range(2):
+                nc.vector.scalar_tensor_tensor(z_t[:, u], fetched[:, u], mu_col[:, b : b + 1], own[b][:, u], ALU.mult, ALU.add)
+                nc.tensor.transpose(z_words[:, u, :], z_t[:, u].rearrange("s p e -> s (p e)").bitcast(F32), ident[:])
+            dst = z_grouped[first][:, 4 * P * (b - first) : 4 * P * (b - first + 1)]
+            copy(dst.bitcast(F32).rearrange("p (s u) -> p s u", u=2), z_words[:].rearrange("p u s -> p s u"))
 
         out_rows = out.rearrange("(m p) s -> p m s", p=P)
-        for b in range(4):
-            z_t = keep.tile([P, H], BF16, name="z_t%d" % b)
-            nc.vector.scalar_tensor_tensor(z_t[:], partner_t[b][:].rearrange("p t m -> p (t m)"), mu_col[:, b : b + 1], own[b][:], ALU.mult, ALU.add)
-            z_words = psum.tile([P, 2, P], F32, name="z_words%d" % b, tag="bank%d" % (4 + b))
-            for u in range(2):
-                nc.tensor.transpose(z_words[:, u, :], z_t[:].bitcast(F32)[:, u : 2 * P : 2], ident[:])
-            z_grouped = keep.tile([P, 4 * P], BF16, name="z_grouped%d" % b, align_bytes=64)
-            nc.scalar.copy(z_grouped[:].bitcast(F32).rearrange("p (s u) -> p s u", u=2), z_words[:].rearrange("p u s -> p s u"))
-            z_q = quantize("z%d" % b, z_grouped[:], P)
-            acc = psum.tile([P, 2, P], F32, name="acc%d" % b, tag="bank%d" % order[b])
+
+        def last_product(b):
+            z_q = quantize("z%d" % b, z_grouped[b][:], P)
+            w2_q = w2_state["q"]
+            for m, copy, queue in ((0, on_scalar, nc.scalar), (1, on_vector, nc.sync)):
+                cols = slice(P * m, P * (m + 1))
+                acc = psum.tile([P, P], F32, name="acc%d%d" % (b, m), tag="bank%d" % (b + 4 * m))
+                nc.tensor.matmul_mx(acc[:], lhsT=w2_q[0][:, cols].bitcast(FP8X4), lhsT_scale=w2_q[1][:, cols],
+                                    rhs=z_q[0][:].bitcast(FP8X4), rhs_scale=z_q[1][:], start=True, stop=True)
+                result = keep.tile([P, P], F32, name="result%d%d" % (b, m))
+                copy(result[:], acc[:])
+                queue.dma_start(out_rows[:, m, P * b : P * (b + 1)], result[:])
+
+        def second_product(b, width, copy, tag=None):
+            z_q = quantize("z%d" % b, z_grouped[b][:], width, tag)
+            w2_q = w2_state["q"]
+            acc = psum.tile([P, 2, width], F32, name="acc%d" % b, tag="bank%d" % b)
             for m in range(2):
                 cols = slice(P * m, P * (m + 1))
                 nc.tensor.matmul_mx(acc[:, m, :], lhsT=w2_q[0][:, cols].bitcast(FP8X4), lhsT_scale=w2_q[1][:, cols],
                                     rhs=z_q[0][:].bitcast(FP8X4), rhs_scale=z_q[1][:], start=True, stop=True)
-            result = keep.tile([P, 2, P], F32, name="result%d" % b)
-            nc.scalar.copy(result[:], acc[:])
-            nc.sync.dma_start(out_rows[:, :, P * b : P * (b + 1)], result[:])
+            result = keep.tile([P, 2, width], F32, name="result%d" % b)
+            copy(result[:], acc[:])
+            nc.sync.dma_start(out_rows[:, :, P * b : P * b + width], result[:])
+
+        pick_on_scalar(1)
+        for n in (0, 2, 3):
+            pick(n, 0, 32)
+        weave(0, 0, 64, on_scalar)
+        pick(4, 0, 32)
+        weave(0, 64, 128, on_vector)
+        quant_x(0)
+        pick_on_scalar(5)
+        pick(6, 0, 32)
+        pick(7, 0, 16)
+        weave(1, 0, 32, on_scalar)
+        pick(7, 16, 32)
+        weave(1, 32, 128, on_vector)
+        cast_w1(0, 0, on_scalar)
+        cast_w1(1, 0, on_scalar)
+        quant_x(1)
+        cast_w1(0, 1, on_scalar)
+        quant_w1(0)
+        cast_w1(1, 1, on_scalar)
+        quant_w1(1)
+        cast_w1(2, 0, on_vector)
+        cast_w1(3, 0, on_vector)
+        cast_w1(2, 1, on_vector)
+        cast_w1(3, 1, on_vector)
+        quant_w1(2)
+        quant_w1(3)
+        hidden(0)
+        hidden(1)
+        hidden(2)
+        hidden(3)
+        cast_w2(on_scalar, "w13_codes")
+
+        for t in range(4):
+            turn_own(t)
+        for b in range(4):
+            scale_own(b)
+        for t in range(4):
+            fetch_partner(t, 0, 2, "w1_grouped%d" % (t + 2) if t < 2 else None)
+            fetch_partner(t, 2, 4, None)
+        quant_w2()
+        for b in range(4):
+            mix(b, b, 128, on_scalar)
+        for b in range(4):
+            second_product(b, 128, on_vector if b == 3 else on_scalar)

@@ -4,7 +4,8 @@ import concourse.mybir as mybir
 from concourse.masks import make_identity
 
 K, T, S, H, N = 1024, 1024, 512, 512, 256
-P = 128
+FLOPS = 2 * K * H * S + 2 * H * N * S
+
 F32 = mybir.dt.float32
 BF16 = mybir.dt.bfloat16
 U32 = mybir.dt.uint32
@@ -13,234 +14,201 @@ U8 = mybir.dt.uint8
 FP8X4 = mybir.dt.float8_e4m3fn_x4
 ACT = mybir.ActivationFunctionType
 ALU = mybir.AluOpType
-FLOPS = 2 * K * H * S + 2 * H * N * S
+
+P = 128
+PACK = 4
+PASSES = K // (P * PACK)
+TILES = H // P
+BLOCKS = S // P
+OUT_HALVES = N // P
+LIST_COLUMN = 16
+RUN = 4
+HALF_S = S // 2
+HALF_H = H // 2
+SCALAR_ROW = 1
 
 
 def tile_picked_mixup_gelu_e_kernel(tc, xT, w1, w2, lam, mu, offs, pos1, out):
     nc = tc.nc
+    on_scalar, on_vector = nc.scalar.copy, nc.vector.tensor_copy
     with ExitStack() as ctx:
         keep = ctx.enter_context(tc.tile_pool(name="keep", bufs=1))
         psum = ctx.enter_context(tc.psum_pool(name="psum", bufs=1))
 
-        def quantize(name, grouped, width, tag=None):
-            codes = keep.tile([P, width], U32, name=name + "_codes", tag=tag or name + "_codes", align_bytes=64)
-            scales = keep.tile([P, width], U8, name=name + "_scales", align_bytes=64)
-            nc.vector.quantize_mx(out=codes[:].bitcast(FP8X4), scales=scales[:], in_=grouped)
-            return codes, scales
-
-        offs_sb = keep.tile([P, S // 16], U16, name="offs_sb")
-        pos_sb = keep.tile([P, S // 16], U16, name="pos_sb")
-        lam_col = keep.tile([P, 4], F32, name="lam_col")
-        mu_col = keep.tile([P, 4], F32, name="mu_col")
-        w2_raw = keep.tile([P, 4, N], F32, name="w2_raw")
-        x_rows = xT.rearrange("(z p j) t -> z j p t", z=2, j=4)
-        x_planes = {}
-        w1_raw = {}
-
-        def load_x(n):
-            x_planes[n] = keep.tile([P, T], F32, name="x_plane%d" % n)
-            nc.sync.dma_start(x_planes[n][:], x_rows[n // 4, n % 4])
-
-        def load_w1_half(a, z):
-            raw = keep.tile([P, 4, 256], F32, name="w1_raw%d%d" % (a, z))
-            nc.sync.dma_start(raw[:], w1.rearrange("(z p j) (a c) -> a z p j c", z=2, j=4, a=2)[a, z])
-            w1_raw[a, z] = raw[:]
-
-        def load_w1_pass(z):
-            raw = keep.tile([P, 4, 512], F32, name="w1_raw%d" % z)
-            nc.sync.dma_start(raw[:], w1.rearrange("(z p j) c -> z p j c", z=2, j=4)[z])
-            for a in range(2):
-                w1_raw[a, z] = raw[:, :, 256 * a : 256 * (a + 1)]
-
-        def load_shares():
-            with nc.allow_non_contiguous_dma(reason="one value a partition"):
-                nc.sync.dma_start(lam_col[:], lam[0].rearrange("(b p) -> p b", p=P))
-                nc.sync.dma_start(mu_col[:], mu[0].rearrange("(b p) -> p b", p=P))
-
+        offs_sb = keep.tile([P, S // LIST_COLUMN], U16, name="offs_sb")
         nc.sync.dma_start(offs_sb[:], offs)
-        load_x(0)
-        load_x(1)
-        load_x(2)
-        load_x(3)
-        load_x(4)
-        load_x(5)
-        load_x(6)
-        load_x(7)
-        load_w1_half(0, 0)
-        load_w1_half(0, 1)
-        load_w1_half(1, 0)
-        load_w1_half(1, 1)
+        x_view = xT.rearrange("(z p j) t -> z j p t", z=PASSES, j=PACK)
+        x_rows = {}
+        for z in range(PASSES):
+            for j in range(PACK):
+                x_rows[z, j] = keep.tile([P, T], F32, name="x_rows%d%d" % (z, j))
+                nc.sync.dma_start(x_rows[z, j][:], x_view[z, j])
+        w1_view = w1.rearrange("(z p j) (a c) -> a z p j c", z=PASSES, j=PACK, c=HALF_H)
+        w1_raw = {}
+        for a in range(H // HALF_H):
+            for z in range(PASSES):
+                w1_raw[a, z] = keep.tile([P, PACK, HALF_H], F32, name="w1_raw%d%d" % (a, z))
+                nc.sync.dma_start(w1_raw[a, z][:], w1_view[a, z])
+        pos_sb = keep.tile([P, S // LIST_COLUMN], U16, name="pos_sb")
         nc.sync.dma_start(pos_sb[:], pos1)
-        nc.sync.dma_start(w2_raw[:], w2.rearrange("(p j) n -> p j n", j=4))
-        load_shares()
+        w2_raw = keep.tile([P, PACK, N], F32, name="w2_raw")
+        nc.sync.dma_start(w2_raw[:], w2.rearrange("(p j) n -> p j n", j=PACK))
+        lam_col = keep.tile([P, BLOCKS], F32, name="lam_col")
+        mu_col = keep.tile([P, BLOCKS], F32, name="mu_col")
+        with nc.allow_non_contiguous_dma(reason="one share to a partition"):
+            nc.sync.dma_start(lam_col[:], lam[0].rearrange("(b p) -> p b", p=P))
+            nc.sync.dma_start(mu_col[:], mu[0].rearrange("(b p) -> p b", p=P))
 
-        warm = keep.tile([P, 1], F32, name="warm")
-        nc.gpsimd.memset(warm[:], 0.0)
+        warm_in = keep.tile([P, 1], F32, name="warm_in")
+        nc.gpsimd.memset(warm_in[:], 0.0)
         warm_out = keep.tile([P, 1], F32, name="warm_out")
-        nc.scalar.activation(warm_out[:], warm[:], ACT.Gelu_apprx_tanh)
+        nc.scalar.activation(warm_out[:], warm_in[:], ACT.Gelu_apprx_tanh)
+
         ident = keep.tile([P, P], F32, name="ident")
         make_identity(nc, ident[:])
-        on_scalar, on_vector, on_gpsimd = nc.scalar.copy, nc.vector.tensor_copy, nc.gpsimd.tensor_copy
 
-        w1_grouped, w1_q, x_q, h, own, z_grouped, w2_state = {}, {}, {}, {}, {}, {}, {}
+        def group(copy, grouped, rows):
+            copy(grouped.rearrange("p (c i j) -> p c j i", i=RUN, j=PACK), rows.rearrange("p j (c i) -> p c j i", i=RUN))
 
-        def cast_w1(t, z, copy):
-            if t not in w1_grouped:
-                w1_grouped[t] = keep.tile([P, 2, 4 * P], BF16, name="w1_grouped%d" % t, tag="w1_grouped%d" % t, align_bytes=64)
-            src = w1_raw[t // 2, z][:, :, P * (t % 2) : P * (t % 2 + 1)]
-            copy(w1_grouped[t][:, z, :].rearrange("p (c i j) -> p c j i", i=4, j=4), src.rearrange("p j (c i) -> p c j i", i=4))
+        def quantize(name, grouped, width):
+            codes = keep.tile([P, width], U32, name=name + "_codes", tag=name + "_codes", align_bytes=64)
+            scales = keep.tile([P, width], U8, name=name + "_scales", align_bytes=64)
+            nc.vector.quantize_mx(out=codes[:].bitcast(FP8X4), scales=scales[:], in_=grouped)
+            return codes[:], scales[:]
 
-        def quant_w1(t):
-            codes, scales = quantize("w1%d" % t, w1_grouped[t][:].rearrange("p z w -> p (z w)"), 2 * P)
-            for z in range(2):
-                w1_q[t, z] = (codes[:, P * z : P * (z + 1)], scales[:, P * z : P * (z + 1)])
+        def product(acc, stationary, moving, start, stop):
+            nc.tensor.matmul_mx(acc, lhsT=stationary[0].bitcast(FP8X4), lhsT_scale=stationary[1],
+                                rhs=moving[0].bitcast(FP8X4), rhs_scale=moving[1], start=start, stop=stop)
 
-        def quant_w1_pass(t, z):
-            codes, scales = quantize("w1%d%d" % (t, z), w1_grouped[t][:, z, :], P)
-            w1_q[t, z] = (codes[:], scales[:])
+        def columns(operand, first):
+            return operand[0][:, first : first + P], operand[1][:, first : first + P]
+
+        picked = [keep.tile([P, PACK, S], BF16, name="picked%d" % z, align_bytes=64) for z in range(PASSES)]
+        x_grouped = [keep.tile([P, PACK * S], BF16, name="x_grouped%d" % z, align_bytes=64) for z in range(PASSES)]
+
+        def pick(z, j, first, count):
+            entries = offs_sb[:, first // LIST_COLUMN : (first + count) // LIST_COLUMN]
+            nc.vector.tensor_copy(picked[z][:, j, first : first + count], x_rows[z, j][:].indirect(entries))
+
+        def pick_on_scalar(z, j):
+            rounded = keep.tile([P, T], BF16, name="x_rounded%d" % z)
+            nc.scalar.copy(rounded[:], x_rows[z, j][:])
+            nc.scalar.activation(picked[z][:, j, :], rounded[:].indirect(offs_sb[:]), ACT.Copy)
+
+        def group_x(copy, z, half):
+            first = half * HALF_S
+            group(copy, x_grouped[z][:, PACK * first : PACK * (first + HALF_S)], picked[z][:, :, first : first + HALF_S])
+
+        pick_on_scalar(0, SCALAR_ROW)
+        for j in range(PACK):
+            if j != SCALAR_ROW:
+                pick(0, j, 0, S)
+        group_x(on_scalar, 0, 0)
+        pick(1, 0, 0, S)
+        group_x(on_vector, 0, 1)
+        x_q = [quantize("x0", x_grouped[0][:], S)]
+        pick_on_scalar(1, SCALAR_ROW)
+        pick(1, 2, 0, S)
+        pick(1, 3, 0, HALF_S)
+        group_x(on_scalar, 1, 0)
+        pick(1, 3, HALF_S, HALF_S)
+        group_x(on_vector, 1, 1)
+
+        w1_grouped = [keep.tile([P, PASSES, PACK * P], BF16, name="w1_grouped%d" % t, tag="w1_grouped%d" % t, align_bytes=64)
+                      for t in range(TILES)]
+        pre = [psum.tile([P, S], F32, name="pre%d" % t, tag="bank%d" % t) for t in range(TILES)]
+        w1_q, h = {}, {}
+
+        def group_w1(copy, t, z):
+            a, first = divmod(P * t, HALF_H)
+            group(copy, w1_grouped[t][:, z, :], w1_raw[a, z][:, :, first : first + P])
+
+        def quantize_w1(t):
+            both = quantize("w1_tile%d" % t, w1_grouped[t][:].rearrange("p z w -> p (z w)"), PASSES * P)
+            for z in range(PASSES):
+                w1_q[t, z] = columns(both, P * z)
 
         def hidden(t):
-            first_product(t, 0)
-            first_product(t, 1)
-            gelu(t)
-
-        def cast_w2(copy, tag):
-            w2_state["grouped"] = keep.tile([P, 4 * N], BF16, name="w2_grouped", tag=tag, align_bytes=64)
-            copy(w2_state["grouped"][:].rearrange("p (c i j) -> p c j i", i=4, j=4), w2_raw[:].rearrange("p j (c i) -> p c j i", i=4))
-
-        def quant_w2():
-            w2_state["q"] = quantize("w2", w2_state["grouped"][:], N)
-
-        picked = [keep.tile([P, 4, S], BF16, name="picked%d" % z, align_bytes=64) for z in range(2)]
-        x_grouped = [keep.tile([P, S * 4], BF16, name="x_grouped%d" % z, align_bytes=64) for z in range(2)]
-
-        def weave(z, lo, hi, copy):
-            src = picked[z][:].rearrange("p j (c i) -> p c j i", i=4)
-            dst = x_grouped[z][:].rearrange("p (c i j) -> p c j i", i=4, j=4)
-            copy(dst[:, lo:hi], src[:, lo:hi])
-
-        def pick(n, lo, hi):
-            nc.vector.tensor_copy(picked[n // 4][:, n % 4, 16 * lo : 16 * hi], x_planes[n][:].indirect(offs_sb[:, lo:hi]))
-
-        def pick_on_scalar(n):
-            rounded = keep.tile([P, T], BF16, name="x_rounded%d" % n)
-            nc.scalar.copy(rounded[:], x_planes[n][:])
-            nc.scalar.activation(picked[n // 4][:, n % 4, :], rounded[:].indirect(offs_sb[:]), ACT.Copy)
-
-        def quant_x(z):
-            x_q[z] = quantize("x%d" % z, x_grouped[z][:], S)
-
-        pre = [psum.tile([P, S], F32, name="pre%d" % t, tag="bank%d" % t) for t in range(4)]
-        own_t = [psum.tile([P, 4, P], F32, name="own_t%d" % b, tag="bank%d" % (4 + b)) for b in range(4)]
-        partner_t = {}
-
-        def first_product(t, z):
-            nc.tensor.matmul_mx(pre[t][:], lhsT=w1_q[t, z][0].bitcast(FP8X4), lhsT_scale=w1_q[t, z][1],
-                                rhs=x_q[z][0][:].bitcast(FP8X4), rhs_scale=x_q[z][1][:], start=(z == 0), stop=(z == 1))
-
-        def gelu(t, tag=None):
-            h[t] = keep.tile([P, S], F32, name="h%d" % t, tag=tag or "h%d" % t)
+            for z in range(PASSES):
+                product(pre[t][:], w1_q[t, z], x_q[z], z == 0, z == PASSES - 1)
+            h[t] = keep.tile([P, S], F32, name="h%d" % t)
             nc.scalar.activation(h[t][:], pre[t][:], ACT.Gelu_apprx_tanh)
 
-        def turn_own(t):
-            for b in range(4):
-                nc.tensor.transpose(own_t[b][:, t, :], h[t][:, P * b : P * (b + 1)], ident[:])
+        group_w1(on_vector, 0, 0)
+        w1_q[0, 0] = quantize("w1_tile0_pass0", w1_grouped[0][:, 0, :], P)
+        x_q.append(quantize("x1", x_grouped[1][:], S))
+        group_w1(on_scalar, 0, 1)
+        w1_q[0, 1] = quantize("w1_tile0_pass1", w1_grouped[0][:, 1, :], P)
+        hidden(0)
+        for z in range(PASSES):
+            group_w1(on_scalar, 1, z)
+        quantize_w1(1)
+        hidden(1)
+        for z in range(PASSES):
+            for t in (2, 3):
+                group_w1(on_scalar if (t, z) == (2, 0) else on_vector, t, z)
+        for t in (2, 3):
+            quantize_w1(t)
+        for t in (2, 3):
+            hidden(t)
 
-        def scale_own(b):
-            own[b] = keep.tile([P, 2, 128, 2], F32, name="own%d" % b, tag="own%d" % b, align_bytes=64)
-            nc.scalar.activation(own[b][:], own_t[b][:].rearrange("s t (p u e) -> s u (t p) e", u=2, e=2), ACT.Copy, scale=lam_col[:, b : b + 1])
+        w2_grouped = keep.tile([P, PACK * N], BF16, name="w2_grouped", tag="w1_tile3_codes", align_bytes=64)
+        group(on_scalar, w2_grouped[:], w2_raw[:])
 
-        partners = {}
+        def by_pairs(block):
+            return block[:].rearrange("s t (p u e) -> s u (t p) e", u=2, e=2)
 
-        def fetch_partner(t, lo, hi, tag):
-            if t not in partners:
-                partners[t] = keep.tile([P, S], F32, name="partner%d" % t, tag=tag or "partner%d" % t, align_bytes=64)
-            partner = partners[t][:, P * lo : P * hi]
-            nc.vector.tensor_copy(partner, h[t][:].indirect(pos_sb[:, 8 * lo : 8 * hi]))
-            for b in range(lo, hi):
-                if b not in partner_t:
-                    partner_t[b] = psum.tile([P, 4, P], F32, name="partner_t%d" % b, tag="bank%d" % b)
-                nc.tensor.transpose(partner_t[b][:, t, :], partner[:, P * (b - lo) : P * (b - lo + 1)], ident[:])
+        def turn(block, tiles, b):
+            for t in range(TILES):
+                nc.tensor.transpose(block[:, t, :], tiles[t][:, P * b : P * (b + 1)], ident[:])
 
-        def mix(b, first, width, copy):
-            if first not in z_grouped:
-                z_grouped[first] = keep.tile([P, 4 * width], BF16, name="z_grouped%d" % first, align_bytes=64)
-            z_t = keep.tile([P, 2, 128, 2], BF16, name="z_t%d" % b)
-            z_words = psum.tile([P, 2, P], F32, name="z_words%d" % b, tag="bank%d" % (4 + b))
-            fetched = partner_t[b][:].rearrange("s t (p u e) -> s u (t p) e", u=2, e=2)
+        own = []
+        for b in range(BLOCKS):
+            own_t = psum.tile([P, TILES, P], F32, name="own_t%d" % b, tag="bank%d" % (TILES + b))
+            turn(own_t, h, b)
+            scaled = keep.tile([P, 2, P, 2], F32, name="own%d" % b, align_bytes=64)
+            nc.scalar.activation(scaled[:], by_pairs(own_t), ACT.Copy, scale=lam_col[:, b : b + 1])
+            own.append(scaled)
+
+        partner = [keep.tile([P, S], F32, name="partner%d" % t, align_bytes=64,
+                             tag="w1_grouped%d" % (t + 2) if t < 2 else "partner%d" % t) for t in range(TILES)]
+        for first in range(0, S, HALF_S):
+            entries = pos_sb[:, first // LIST_COLUMN : (first + HALF_S) // LIST_COLUMN]
+            for t in range(TILES):
+                nc.vector.tensor_copy(partner[t][:, first : first + HALF_S], h[t][:].indirect(entries))
+        partner_t = []
+        for b in range(BLOCKS):
+            partner_t.append(psum.tile([P, TILES, P], F32, name="partner_t%d" % b, tag="bank%d" % b))
+            turn(partner_t[b], partner, b)
+
+        w2_q = quantize("w2", w2_grouped[:], N)
+
+        z_grouped = []
+        for b in range(BLOCKS):
+            z_grouped.append(keep.tile([P, PACK * P], BF16, name="z_grouped%d" % b, align_bytes=64))
+            z_t = keep.tile([P, 2, P, 2], BF16, name="z_t%d" % b)
+            z_words = psum.tile([P, 2, P], F32, name="z_words%d" % b, tag="bank%d" % (TILES + b))
             for u in range(2):
-                nc.vector.scalar_tensor_tensor(z_t[:, u], fetched[:, u], mu_col[:, b : b + 1], own[b][:, u], ALU.mult, ALU.add)
+                nc.vector.scalar_tensor_tensor(z_t[:, u], by_pairs(partner_t[b])[:, u], mu_col[:, b : b + 1], own[b][:, u],
+                                               ALU.mult, ALU.add)
                 nc.tensor.transpose(z_words[:, u, :], z_t[:, u].rearrange("s p e -> s (p e)").bitcast(F32), ident[:])
-            dst = z_grouped[first][:, 4 * P * (b - first) : 4 * P * (b - first + 1)]
-            copy(dst.bitcast(F32).rearrange("p (s u) -> p s u", u=2), z_words[:].rearrange("p u s -> p s u"))
+            nc.scalar.copy(z_grouped[b][:].bitcast(F32).rearrange("p (s u) -> p s u", u=2), z_words[:].rearrange("p u s -> p s u"))
 
         out_rows = out.rearrange("(m p) s -> p m s", p=P)
-
-        def last_product(b):
+        for b in range(BLOCKS - 1):
             z_q = quantize("z%d" % b, z_grouped[b][:], P)
-            w2_q = w2_state["q"]
-            for m, copy, queue in ((0, on_scalar, nc.scalar), (1, on_vector, nc.sync)):
-                cols = slice(P * m, P * (m + 1))
-                acc = psum.tile([P, P], F32, name="acc%d%d" % (b, m), tag="bank%d" % (b + 4 * m))
-                nc.tensor.matmul_mx(acc[:], lhsT=w2_q[0][:, cols].bitcast(FP8X4), lhsT_scale=w2_q[1][:, cols],
-                                    rhs=z_q[0][:].bitcast(FP8X4), rhs_scale=z_q[1][:], start=True, stop=True)
-                result = keep.tile([P, P], F32, name="result%d%d" % (b, m))
-                copy(result[:], acc[:])
-                queue.dma_start(out_rows[:, m, P * b : P * (b + 1)], result[:])
+            acc = psum.tile([P, OUT_HALVES, P], F32, name="acc%d" % b, tag="bank%d" % b)
+            for m in range(OUT_HALVES):
+                product(acc[:, m, :], columns(w2_q, P * m), z_q, True, True)
+            result = keep.tile([P, OUT_HALVES, P], F32, name="result%d" % b)
+            nc.scalar.copy(result[:], acc[:])
+            nc.sync.dma_start(out_rows[:, :, P * b : P * (b + 1)], result[:])
 
-        def second_product(b, width, copy, tag=None):
-            z_q = quantize("z%d" % b, z_grouped[b][:], width, tag)
-            w2_q = w2_state["q"]
-            acc = psum.tile([P, 2, width], F32, name="acc%d" % b, tag="bank%d" % b)
-            for m in range(2):
-                cols = slice(P * m, P * (m + 1))
-                nc.tensor.matmul_mx(acc[:, m, :], lhsT=w2_q[0][:, cols].bitcast(FP8X4), lhsT_scale=w2_q[1][:, cols],
-                                    rhs=z_q[0][:].bitcast(FP8X4), rhs_scale=z_q[1][:], start=True, stop=True)
-            result = keep.tile([P, 2, width], F32, name="result%d" % b)
+        last = BLOCKS - 1
+        z_q = quantize("z%d" % last, z_grouped[last][:], P)
+        for m, copy, queue in ((0, on_scalar, nc.scalar), (1, on_vector, nc.sync)):
+            acc = psum.tile([P, P], F32, name="acc_last%d" % m, tag="bank%d" % (last + TILES * m))
+            product(acc[:], columns(w2_q, P * m), z_q, True, True)
+            result = keep.tile([P, P], F32, name="result_last%d" % m)
             copy(result[:], acc[:])
-            nc.sync.dma_start(out_rows[:, :, P * b : P * b + width], result[:])
-
-        pick_on_scalar(1)
-        for n in (0, 2, 3):
-            pick(n, 0, 32)
-        weave(0, 0, 64, on_scalar)
-        pick(4, 0, 32)
-        weave(0, 64, 128, on_vector)
-        quant_x(0)
-        pick_on_scalar(5)
-        pick(6, 0, 32)
-        pick(7, 0, 16)
-        weave(1, 0, 32, on_scalar)
-        pick(7, 16, 32)
-        weave(1, 32, 128, on_vector)
-        cast_w1(0, 0, on_scalar)
-        cast_w1(1, 0, on_scalar)
-        quant_x(1)
-        cast_w1(0, 1, on_scalar)
-        quant_w1(0)
-        cast_w1(1, 1, on_scalar)
-        quant_w1(1)
-        cast_w1(2, 0, on_vector)
-        cast_w1(3, 0, on_vector)
-        cast_w1(2, 1, on_vector)
-        cast_w1(3, 1, on_vector)
-        quant_w1(2)
-        quant_w1(3)
-        hidden(0)
-        hidden(1)
-        hidden(2)
-        hidden(3)
-        cast_w2(on_scalar, "w13_codes")
-
-        for t in range(4):
-            turn_own(t)
-        for b in range(4):
-            scale_own(b)
-        for t in range(4):
-            fetch_partner(t, 0, 2, "w1_grouped%d" % (t + 2) if t < 2 else None)
-            fetch_partner(t, 2, 4, None)
-        quant_w2()
-        for b in range(4):
-            mix(b, b, 128, on_scalar)
-        for b in range(4):
-            second_product(b, 128, on_vector if b == 3 else on_scalar)
+            queue.dma_start(out_rows[:, m, P * last : P * (last + 1)], result[:])

from contextlib import ExitStack

import concourse.mybir as mybir
from concourse.masks import make_identity

K, T, S, H, N = 1024, 1024, 512, 512, 256
FLOPS = 2 * K * H * S + 2 * H * N * S

F32 = mybir.dt.float32
BF16 = mybir.dt.bfloat16
U32 = mybir.dt.uint32
U16 = mybir.dt.uint16
U8 = mybir.dt.uint8
FP8X4 = mybir.dt.float8_e4m3fn_x4
ACT = mybir.ActivationFunctionType
ALU = mybir.AluOpType

P = 128
PACK = 4
PASSES = K // (P * PACK)
TILES = H // P
BLOCKS = S // P
OUT_HALVES = N // P
LIST_COLUMN = 16
RUN = 4
HALF_S = S // 2
HALF_H = H // 2
SCALAR_ROW = 1


def tile_picked_mixup_gelu_e_kernel(tc, xT, w1, w2, lam, mu, offs, pos1, out):
    nc = tc.nc
    on_scalar, on_vector = nc.scalar.copy, nc.vector.tensor_copy
    with ExitStack() as ctx:
        keep = ctx.enter_context(tc.tile_pool(name="keep", bufs=1))
        psum = ctx.enter_context(tc.psum_pool(name="psum", bufs=1))

        offs_sb = keep.tile([P, S // LIST_COLUMN], U16, name="offs_sb")
        nc.sync.dma_start(offs_sb[:], offs)
        x_view = xT.rearrange("(z p j) t -> z j p t", z=PASSES, j=PACK)
        x_rows = {}
        for z in range(PASSES):
            for j in range(PACK):
                x_rows[z, j] = keep.tile([P, T], F32, name="x_rows%d%d" % (z, j))
                nc.sync.dma_start(x_rows[z, j][:], x_view[z, j])
        w1_view = w1.rearrange("(z p j) (a c) -> a z p j c", z=PASSES, j=PACK, c=HALF_H)
        w1_raw = {}
        for a in range(H // HALF_H):
            for z in range(PASSES):
                w1_raw[a, z] = keep.tile([P, PACK, HALF_H], F32, name="w1_raw%d%d" % (a, z))
                nc.sync.dma_start(w1_raw[a, z][:], w1_view[a, z])
        pos_sb = keep.tile([P, S // LIST_COLUMN], U16, name="pos_sb")
        nc.sync.dma_start(pos_sb[:], pos1)
        w2_raw = keep.tile([P, PACK, N], F32, name="w2_raw")
        nc.sync.dma_start(w2_raw[:], w2.rearrange("(p j) n -> p j n", j=PACK))
        lam_col = keep.tile([P, BLOCKS], F32, name="lam_col")
        mu_col = keep.tile([P, BLOCKS], F32, name="mu_col")
        with nc.allow_non_contiguous_dma(reason="one share to a partition"):
            nc.sync.dma_start(lam_col[:], lam[0].rearrange("(b p) -> p b", p=P))
            nc.sync.dma_start(mu_col[:], mu[0].rearrange("(b p) -> p b", p=P))

        warm_in = keep.tile([P, 1], F32, name="warm_in")
        nc.gpsimd.memset(warm_in[:], 0.0)
        warm_out = keep.tile([P, 1], F32, name="warm_out")
        nc.scalar.activation(warm_out[:], warm_in[:], ACT.Gelu_apprx_tanh)

        ident = keep.tile([P, P], F32, name="ident")
        make_identity(nc, ident[:])

        def group(copy, grouped, rows):
            copy(grouped.rearrange("p (c i j) -> p c j i", i=RUN, j=PACK), rows.rearrange("p j (c i) -> p c j i", i=RUN))

        def quantize(name, grouped, width):
            codes = keep.tile([P, width], U32, name=name + "_codes", tag=name + "_codes", align_bytes=64)
            scales = keep.tile([P, width], U8, name=name + "_scales", align_bytes=64)
            nc.vector.quantize_mx(out=codes[:].bitcast(FP8X4), scales=scales[:], in_=grouped)
            return codes[:], scales[:]

        def product(acc, stationary, moving, start, stop):
            nc.tensor.matmul_mx(acc, lhsT=stationary[0].bitcast(FP8X4), lhsT_scale=stationary[1],
                                rhs=moving[0].bitcast(FP8X4), rhs_scale=moving[1], start=start, stop=stop)

        def columns(operand, first):
            return operand[0][:, first : first + P], operand[1][:, first : first + P]

        picked = [keep.tile([P, PACK, S], BF16, name="picked%d" % z, align_bytes=64) for z in range(PASSES)]
        x_grouped = [keep.tile([P, PACK * S], BF16, name="x_grouped%d" % z, align_bytes=64) for z in range(PASSES)]

        def pick(z, j, first, count):
            entries = offs_sb[:, first // LIST_COLUMN : (first + count) // LIST_COLUMN]
            nc.vector.tensor_copy(picked[z][:, j, first : first + count], x_rows[z, j][:].indirect(entries))

        def pick_on_scalar(z, j):
            rounded = keep.tile([P, T], BF16, name="x_rounded%d" % z)
            nc.scalar.copy(rounded[:], x_rows[z, j][:])
            nc.scalar.activation(picked[z][:, j, :], rounded[:].indirect(offs_sb[:]), ACT.Copy)

        def group_x(copy, z, half):
            first = half * HALF_S
            group(copy, x_grouped[z][:, PACK * first : PACK * (first + HALF_S)], picked[z][:, :, first : first + HALF_S])

        pick_on_scalar(0, SCALAR_ROW)
        for j in range(PACK):
            if j != SCALAR_ROW:
                pick(0, j, 0, S)
        group_x(on_scalar, 0, 0)
        pick(1, 0, 0, S)
        group_x(on_vector, 0, 1)
        x_q = [quantize("x0", x_grouped[0][:], S)]
        pick_on_scalar(1, SCALAR_ROW)
        pick(1, 2, 0, S)
        pick(1, 3, 0, HALF_S)
        group_x(on_scalar, 1, 0)
        pick(1, 3, HALF_S, HALF_S)
        group_x(on_vector, 1, 1)

        w1_grouped = [keep.tile([P, PASSES, PACK * P], BF16, name="w1_grouped%d" % t, tag="w1_grouped%d" % t, align_bytes=64)
                      for t in range(TILES)]
        pre = [psum.tile([P, S], F32, name="pre%d" % t, tag="bank%d" % t) for t in range(TILES)]
        w1_q, h = {}, {}

        def group_w1(copy, t, z):
            a, first = divmod(P * t, HALF_H)
            group(copy, w1_grouped[t][:, z, :], w1_raw[a, z][:, :, first : first + P])

        def quantize_w1(t):
            both = quantize("w1_tile%d" % t, w1_grouped[t][:].rearrange("p z w -> p (z w)"), PASSES * P)
            for z in range(PASSES):
                w1_q[t, z] = columns(both, P * z)

        def hidden(t):
            for z in range(PASSES):
                product(pre[t][:], w1_q[t, z], x_q[z], z == 0, z == PASSES - 1)
            h[t] = keep.tile([P, S], F32, name="h%d" % t)
            nc.scalar.activation(h[t][:], pre[t][:], ACT.Gelu_apprx_tanh)

        group_w1(on_vector, 0, 0)
        w1_q[0, 0] = quantize("w1_tile0_pass0", w1_grouped[0][:, 0, :], P)
        x_q.append(quantize("x1", x_grouped[1][:], S))
        group_w1(on_scalar, 0, 1)
        w1_q[0, 1] = quantize("w1_tile0_pass1", w1_grouped[0][:, 1, :], P)
        hidden(0)
        for z in range(PASSES):
            group_w1(on_scalar, 1, z)
        quantize_w1(1)
        hidden(1)
        for z in range(PASSES):
            for t in (2, 3):
                group_w1(on_scalar if (t, z) == (2, 0) else on_vector, t, z)
        for t in (2, 3):
            quantize_w1(t)
        for t in (2, 3):
            hidden(t)

        w2_grouped = keep.tile([P, PACK * N], BF16, name="w2_grouped", tag="w1_tile3_codes", align_bytes=64)
        group(on_scalar, w2_grouped[:], w2_raw[:])

        def by_pairs(block):
            return block[:].rearrange("s t (p u e) -> s u (t p) e", u=2, e=2)

        def turn(block, tiles, b):
            for t in range(TILES):
                nc.tensor.transpose(block[:, t, :], tiles[t][:, P * b : P * (b + 1)], ident[:])

        own = []
        for b in range(BLOCKS):
            own_t = psum.tile([P, TILES, P], F32, name="own_t%d" % b, tag="bank%d" % (TILES + b))
            turn(own_t, h, b)
            scaled = keep.tile([P, 2, P, 2], F32, name="own%d" % b, align_bytes=64)
            nc.scalar.activation(scaled[:], by_pairs(own_t), ACT.Copy, scale=lam_col[:, b : b + 1])
            own.append(scaled)

        partner = [keep.tile([P, S], F32, name="partner%d" % t, align_bytes=64,
                             tag="w1_grouped%d" % (t + 2) if t < 2 else "partner%d" % t) for t in range(TILES)]
        for first in range(0, S, HALF_S):
            entries = pos_sb[:, first // LIST_COLUMN : (first + HALF_S) // LIST_COLUMN]
            for t in range(TILES):
                nc.vector.tensor_copy(partner[t][:, first : first + HALF_S], h[t][:].indirect(entries))
        partner_t = []
        for b in range(BLOCKS):
            partner_t.append(psum.tile([P, TILES, P], F32, name="partner_t%d" % b, tag="bank%d" % b))
            turn(partner_t[b], partner, b)

        w2_q = quantize("w2", w2_grouped[:], N)

        z_grouped = []
        for b in range(BLOCKS):
            z_grouped.append(keep.tile([P, PACK * P], BF16, name="z_grouped%d" % b, align_bytes=64))
            z_t = keep.tile([P, 2, P, 2], BF16, name="z_t%d" % b)
            z_words = psum.tile([P, 2, P], F32, name="z_words%d" % b, tag="bank%d" % (TILES + b))
            for u in range(2):
                nc.vector.scalar_tensor_tensor(z_t[:, u], by_pairs(partner_t[b])[:, u], mu_col[:, b : b + 1], own[b][:, u],
                                               ALU.mult, ALU.add)
                nc.tensor.transpose(z_words[:, u, :], z_t[:, u].rearrange("s p e -> s (p e)").bitcast(F32), ident[:])
            nc.scalar.copy(z_grouped[b][:].bitcast(F32).rearrange("p (s u) -> p s u", u=2), z_words[:].rearrange("p u s -> p s u"))

        out_rows = out.rearrange("(m p) s -> p m s", p=P)
        for b in range(BLOCKS - 1):
            z_q = quantize("z%d" % b, z_grouped[b][:], P)
            acc = psum.tile([P, OUT_HALVES, P], F32, name="acc%d" % b, tag="bank%d" % b)
            for m in range(OUT_HALVES):
                product(acc[:, m, :], columns(w2_q, P * m), z_q, True, True)
            result = keep.tile([P, OUT_HALVES, P], F32, name="result%d" % b)
            nc.scalar.copy(result[:], acc[:])
            nc.sync.dma_start(out_rows[:, :, P * b : P * (b + 1)], result[:])

        last = BLOCKS - 1
        z_q = quantize("z%d" % last, z_grouped[last][:], P)
        for m, copy, queue in ((0, on_scalar, nc.scalar), (1, on_vector, nc.sync)):
            acc = psum.tile([P, P], F32, name="acc_last%d" % m, tag="bank%d" % (last + TILES * m))
            product(acc[:], columns(w2_q, P * m), z_q, True, True)
            result = keep.tile([P, P], F32, name="result_last%d" % m)
            copy(result[:], acc[:])
            queue.dma_start(out_rows[:, m, P * last : P * (last + 1)], result[:])
